import numpy as np
import ml_dtypes


def mxq(x, axis, fmt="e4m3"):
    dtype, down = {"e4m3": (ml_dtypes.float8_e4m3fn, 7), "e5m2": (ml_dtypes.float8_e5m2, 14)}[fmt]
    v = np.moveaxis(np.asarray(x, np.float32).astype(ml_dtypes.bfloat16).astype(np.float64), axis, -1)
    blocks = v.reshape(v.shape[:-1] + (-1, 32))
    amax = np.abs(blocks).max(-1, keepdims=True)
    byte = np.maximum(np.where(amax > 0, np.frexp(amax)[1] - 1 + 127, 0) - down, 1)
    scale = np.exp2(byte - 127.0)
    codes = (blocks / scale).astype(np.float32).astype(dtype).astype(np.float64)
    return np.moveaxis((codes * scale).reshape(v.shape), -1, axis)


WIDE = False


def mx_kscale(k):
    if not WIDE:
        return np.ones(k)
    levels = np.array([10, -10, 5, -5, 0])
    if k % 512:
        return np.exp2(np.random.permutation(np.resize(levels, k // 32))).repeat(32)
    a = np.empty((k // 512, 16))
    for p in range(k // 512):
        a[p, :8] = np.random.permutation(np.resize(levels, 8))
        for g in range(8):
            far = levels[np.abs(levels - a[p, g]) >= 10]
            a[p, g + 8] = far[np.random.randint(len(far))]
    return np.exp2(a.ravel()).repeat(32)


def f64(x):
    return np.asarray(x).astype(np.float64)


def striped(idx):
    return np.tile(idx.reshape(-1, 16).T, (8, 1)).astype(np.uint16)


def unstriped(offs):
    return offs[:16].T.reshape(-1).astype(np.int64)


def striped8(idx):
    return np.concatenate([x.reshape(-1, 16).T for x in idx]).astype(np.uint16)


def runs(offs, k):
    lists = np.stack([offs[16 * r : 16 * r + 16].T.reshape(-1) for r in range(8)]).astype(np.int64)
    return lists[np.arange(k) % 512 // 64]


def pack_weight(w):
    k, n = w.shape
    w = f64(np.asarray(w, np.float32).astype(ml_dtypes.bfloat16)).reshape(k // 32, 32, n)
    amax = np.abs(w).max(1)
    byte = np.clip(np.where(amax > 0, np.frexp(amax)[1] - 1 + 127 - 7, 1), 1, 254)
    scaled = (w * np.exp2(127.0 - byte)[:, None, :]).reshape(k, n).astype(np.float32)
    words = np.ascontiguousarray(scaled.reshape(k // 512, 128, 4, n).transpose(0, 1, 3, 2)).astype(ml_dtypes.float8_e4m3fn).view(np.uint8)
    return words, np.ascontiguousarray(byte.astype(np.uint8).reshape(k // 512, 16, n))


def unpack_weight(words, scales):
    g, p, n, _ = words.shape
    vals = np.ascontiguousarray(words).view(ml_dtypes.float8_e4m3fn).astype(np.float64) * np.repeat(np.exp2(scales.astype(np.float64) - 127.0), 8, axis=1)[..., None]
    return vals.transpose(0, 1, 3, 2).reshape(g * 512, n)


K, T, S, N, G, H, W, U = 512, 2048, 512, 512, 2048, 512, 1024, 384


def setup_inputs():
    n = np.random.standard_normal
    s = mx_kscale(K)[:, None]
    u = mx_kscale(S)
    packed_xT = pack_weight(n((K, T)) * s)
    packed_dT = pack_weight(n((K, G)) / s)
    return {
        "x_words": packed_xT[0],
        "x_scales": packed_xT[1],
        "d_words": packed_dT[0],
        "d_scales": packed_dT[1],
        "gn": (np.random.uniform(0.5, 1.5, (H, 1)) * u[:, None]).astype(np.float32),
        "w1": (n((H, N)) / np.sqrt(2 * H) / u[:, None]).astype(np.float32),
        "w2": (n((K, N)) / np.sqrt(2 * K) / s).astype(np.float32),
        "offs": striped(np.random.permutation(T)[:S]),
        "k1": striped8(np.random.randint(0, G, (8, H))),
        "n1": striped(np.random.randint(0, S, W)),
        "two": striped(np.random.permutation(T)[:S]),
        "n2": striped(np.random.permutation(S)[:U]),
        "n3": striped(np.random.permutation(S)[:U]),
    }


def reference(x_words, x_scales, d_words, d_scales, gn, w1, w2, offs, k1, n1, two, n2, n3):
    d_k1 = unpack_weight(d_words, d_scales)[np.arange(K)[:, None], runs(k1, K)]
    xq = unpack_weight(x_words, x_scales)[:, unstriped(offs)]
    s = 0.0625 * (d_k1.T @ xq)
    mb = s[:, unstriped(n1)]
    ms = mb.reshape(H, S, 2).sum(axis=2)
    mx = mb.reshape(H, S, 2).max(axis=2)
    z = f64(gn) * (ms - np.maximum(s, mx))
    x_two = unpack_weight(x_words, x_scales)[:, unstriped(two)]
    h = mxq(f64(w1), 0, "e4m3").T @ mxq(z, 0, "e4m3") + mxq(f64(w2), 0, "e4m3").T @ x_two
    old = h[:, unstriped(n2)]
    pa = h[:, unstriped(n3)]
    ra = old - (0.5 * pa)
    out = h.copy()
    out[:, unstriped(n2)] = ra
    return out

@@ -1,0 +1,212 @@
+from contextlib import ExitStack
+
+import concourse.mybir as mybir
+
+K, T, S, N, G, H, W, U = 512, 2048, 512, 512, 2048, 512, 1024, 384
+FLOPS = 2 * K * H * S + 2 * H * N * S + 2 * K * N * S
+
+F32 = mybir.dt.float32
+BF16 = mybir.dt.bfloat16
+I32 = mybir.dt.int32
+U32 = mybir.dt.uint32
+U16 = mybir.dt.uint16
+U8 = mybir.dt.uint8
+FP8X4 = mybir.dt.float8_e4m3fn_x4
+ALU = mybir.AluOpType
+COPY = mybir.ActivationFunctionType.Copy
+
+P = 128
+PACK = 4
+LIST_ROWS = 16
+BLOCKS = 16
+RUN = 4
+VECTOR_GATHERS = 3
+CHUNKS = (128, 256, 128)
+SCORE_SPARE = 32
+OUT_SPARE = 256
+
+
+def tile_picked_kmixgpairkdif_none_p_kernel(
+    tc, x_words, x_scales, d_words, d_scales, gn, w1, w2, offs, k1, n1, two, n2, n3, out
+):
+    nc = tc.nc
+    with ExitStack() as ctx:
+        keep = ctx.enter_context(tc.tile_pool(name="keep", bufs=1))
+        psum = ctx.enter_context(tc.psum_pool(name="psum", bufs=1))
+
+        def tile(name, shape, dtype, tag=None):
+            return keep.tile(shape, dtype, name=name, tag=tag or name, align_bytes=64)
+
+        def load_list(name, source):
+            offsets = tile(name, list(source.shape), U16)
+            nc.sync.dma_start(offsets[:], source)
+            return offsets
+
+        def load_words(name, source):
+            words = tile(name, [P, source.shape[2]], I32)
+            nc.sync.dma_start(words[:], source[0].rearrange("p n t -> p (n t)").bitcast(I32))
+            return words
+
+        def gather(name, window, offsets, dtype):
+            picked = tile(name, [P, offsets.shape[1] * LIST_ROWS], dtype)
+            nc.vector.tensor_copy(picked[:], window.indirect(offsets[:]))
+            return picked
+
+        def deal(name, source, dtype):
+            dealt = tile(name, [P, H], dtype)
+            nc.vector.tensor_copy(
+                dealt[:].bitcast(U32).rearrange("p (t g r) -> p t g r", t=PACK, g=BLOCKS),
+                source[:].bitcast(U32).rearrange("p (g t r) -> p t g r", t=PACK, g=BLOCKS),
+            )
+            return dealt
+
+        def word_order(grouped):
+            return grouped[:].rearrange("p (c i t) -> p c t i", i=RUN, t=PACK)
+
+        def plane_order(planes):
+            return planes.rearrange("p t (c i) -> p c t i", i=RUN)
+
+        def quantize(name, grouped):
+            width = grouped.shape[1] // PACK
+            codes = tile(name + "_codes", [P, width], U32)
+            scales = tile(name + "_scales", [P, width], U8)
+            nc.vector.quantize_mx(out=codes[:].bitcast(FP8X4), scales=scales[:], in_=grouped[:])
+            return codes, scales
+
+        def multiply(acc, left, left_cols, right, right_cols, start, stop):
+            nc.tensor.matmul_mx(
+                out=acc,
+                lhsT=left[0][:, left_cols].bitcast(FP8X4),
+                lhsT_scale=left[1][:, left_cols],
+                rhs=right[0][:, right_cols].bitcast(FP8X4),
+                rhs_scale=right[1][:, right_cols],
+                start=start,
+                stop=stop,
+            )
+
+        k1_sb = load_list("k1_sb", k1)
+        d_scale_table = tile("d_scale_table", [P, G], U8)
+        nc.sync.dma_start(
+            d_scale_table[:].bitcast(I32), d_scales[0].bitcast(I32).unsqueeze(1).broadcast_to([16, 8, G // 4])
+        )
+        offs_sb = load_list("offs_sb", offs)
+        two_sb = load_list("two_sb", two)
+        n1_sb = load_list("n1_sb", n1)
+        n3_sb = load_list("n3_sb", n3)
+        n2_sb = load_list("n2_sb", n2)
+        d_word_table = load_words("d_word_table", d_words)
+        x_word_table = load_words("x_word_table", x_words)
+        x_scale_table = tile("x_scale_table", [P, T], U8)
+        nc.vector.memset(x_scale_table[:].bitcast(I32), 0)
+        for q in range(4):
+            nc.scalar.dma_start(
+                x_scale_table[32 * q : 32 * q + 4, :].bitcast(I32), x_scales[0, 4 * q : 4 * q + 4, :].bitcast(I32)
+            )
+
+        scores = [tile(f"scores{t}", [P, S + SCORE_SPARE], F32) for t in range(PACK)]
+        for t in range(PACK):
+            nc.gpsimd.memset(scores[t][:, S:], 0.0)
+        results = [tile(f"results{m}", [P, S + OUT_SPARE * (1 - m % 2)], F32) for m in range(N // P)]
+        for m in range(0, N // P, 2):
+            nc.gpsimd.memset(results[m][:, S:], 0.0)
+
+        key_scales_picked = gather("key_scales_picked", d_scale_table[:], k1_sb, U8)
+        key_scales = deal("key_scales", key_scales_picked, U8)
+        for i in range(1, 4):
+            nc.scalar.dma_start(key_scales[i:P:32, :].bitcast(I32), key_scales[8 * i : P : 32, :].bitcast(I32))
+        token_scales = gather("token_scales", x_scale_table[:], offs_sb, U8)
+        key_words_picked = gather("key_words_picked", d_word_table[:].bitcast(U32), k1_sb, U32)
+        key_words = deal("key_words", key_words_picked, U32)
+        w2_raw = tile("w2_raw", [P, PACK, N], F32, tag="d_word_table")
+        nc.sync.dma_start(w2_raw[:], w2.rearrange("(p t) n -> p t n", t=PACK))
+        gains = tile("gains", [P, PACK, 8], F32, tag="key_words_picked")
+        for t in range(PACK):
+            nc.sync.dma_start(gains[:, t, 0:1], gn.rearrange("(g t r) o -> t g r o", t=PACK, g=BLOCKS)[t])
+        token_words = gather("token_words", x_word_table[:].bitcast(U32), offs_sb, U32)
+
+        for t in range(PACK):
+            acc = psum.tile([P, S], F32, name=f"score_acc{t}", tag=f"bank{t}")
+            multiply(acc[:], (key_words, key_scales), slice(t * P, (t + 1) * P), (token_words, token_scales), slice(0, S), True, True)
+            nc.scalar.activation(scores[t][:, :S], acc[:], COPY, scale=0.0625)
+
+        second = (
+            gather("second_words", x_word_table[:].bitcast(U32), two_sb, U32),
+            gather("second_scales", x_scale_table[:], two_sb, U8),
+        )
+
+        w1_raw = tile("w1_raw", [P, PACK, N], F32, tag="x_scale_table")
+        for t in range(PACK):
+            nc.sync.dma_start(w1_raw[:, t, :], w1.rearrange("(g t r) n -> t g r n", t=PACK, g=BLOCKS)[t])
+        w2_grouped = tile("w2_grouped", [P, PACK * N], BF16)
+        nc.vector.tensor_copy(word_order(w2_grouped), plane_order(w2_raw[:]))
+        w2_mx = quantize("w2", w2_grouped)
+
+        spans = []
+        for width in CHUNKS:
+            first = sum(span.stop - span.start for span in spans)
+            spans.append(slice(first, first + width))
+        last = len(spans) - 1
+        early = spans[last].start
+
+        w1_grouped = tile("w1_grouped", [P, PACK * N], BF16)
+        members = []
+        for c, cols in enumerate(spans):
+            pair_offsets = n1_sb[:, 2 * cols.start // LIST_ROWS : 2 * cols.stop // LIST_ROWS]
+            members.append(tile(f"members{c}", [P, PACK, 2 * CHUNKS[c]], F32))
+            if c == last:
+                nc.scalar.copy(word_order(w1_grouped), plane_order(w1_raw[:]))
+            for t in range(PACK):
+                if c == 0 and t < VECTOR_GATHERS:
+                    nc.vector.tensor_copy(members[c][:, t, :], scores[t][:].indirect(pair_offsets))
+                else:
+                    nc.scalar.activation(members[c][:, t, :], scores[t][:].indirect(pair_offsets), COPY)
+
+        z_mx = []
+        for c, cols in enumerate(spans):
+            width = CHUNKS[c]
+            larger = tile(f"larger{c}", [P, PACK, width], F32)
+            pairs = members[c][:].rearrange("p t (j e) -> p t j e", e=2)
+            for t in range(PACK):
+                nc.vector.tensor_tensor(larger[:, t, :], pairs[:, t, :, 0], scores[t][:, cols], ALU.max)
+            excess = tile(f"excess{c}", [P, PACK, width], F32)
+            nc.vector.tensor_tensor(excess[:], pairs[:, :, :, 1], larger[:], ALU.subtract)
+            rest = tile(f"rest{c}", [P, PACK, width], F32)
+            nc.vector.scalar_tensor_tensor(rest[:], excess[:], 0.0, pairs[:, :, :, 0], ALU.min, ALU.add)
+            z_grouped = tile(f"z_grouped{c}", [P, PACK * width], BF16)
+            spread_gains = gains[:, :, 0:1].unsqueeze(1).broadcast_to([P, width // RUN, PACK, RUN])
+            nc.vector.tensor_tensor(word_order(z_grouped), plane_order(rest[:]), spread_gains, ALU.mult)
+            z_mx.append(quantize(f"z{c}", z_grouped))
+            if c == last - 1:
+                w1_mx = quantize("w1", w1_grouped)
+
+        order = (1, 0, 3, 2)
+        early_acc = {m: psum.tile([P, early], F32, name=f"early_acc{m}", tag=f"bank{PACK + m}") for m in order}
+        last_acc = {m: psum.tile([P, S - early], F32, name=f"last_acc{m}", tag=f"bank{m}") for m in order}
+
+        def target(c, m):
+            return last_acc[m][:] if c == last else early_acc[m][:, spans[c]]
+
+        for m in order:
+            for c, cols in enumerate(spans):
+                multiply(target(c, m), w2_mx, slice(m * P, (m + 1) * P), second, cols, c in (0, last), False)
+        for c, cols in enumerate(spans):
+            for m in order:
+                multiply(target(c, m), w1_mx, slice(m * P, (m + 1) * P), z_mx[c], slice(0, CHUNKS[c]), False, c >= last - 1)
+                if c == last - 1:
+                    nc.scalar.copy(results[m][:, :early], early_acc[m][:])
+                if c == last:
+                    (nc.scalar.copy if m % 2 else nc.vector.tensor_copy)(results[m][:, early:S], last_acc[m][:])
+
+        partners = {}
+        for m in (1, 0, 3, 2):
+            partners[m] = tile(f"partner{m}", [P, U], F32)
+            nc.scalar.activation(partners[m][:], results[m][:].indirect(n3_sb[:]), COPY, scale=-0.5)
+        for m in (0, 2):
+            old = tile(f"old{m}", [P, U], F32)
+            nc.vector.tensor_copy(old[:], results[m][:].indirect(n2_sb[:]))
+            new = tile(f"new{m + 1}", [P, U], F32)
+            nc.vector.tensor_tensor(new[:], results[m + 1][:].indirect(n2_sb[:]), partners[m + 1][:], ALU.add)
+            nc.scalar.activation(results[m + 1][:].indirect(n2_sb[:]), new[:], COPY)
+            nc.vector.tensor_tensor(results[m][:].indirect(n2_sb[:]), old[:], partners[m][:], ALU.add)
+        for m in range(N // P):
+            nc.sync.dma_start(out[m * P : (m + 1) * P, :], results[m][:, :S])

@@ -20,7 +20,6 @@ PACK = 4
 LIST_ROWS = 16
 BLOCKS = 16
 RUN = 4
-VECTOR_GATHERS = 3
 CHUNKS = (128, 256, 128)
 SCORE_SPARE = 32
 OUT_SPARE = 256
@@ -47,18 +46,16 @@ def tile_picked_kmixgpairkdif_none_p_kernel(
             nc.sync.dma_start(words[:], source[0].rearrange("p n t -> p (n t)").bitcast(I32))
             return words
 
-        def gather(name, window, offsets, dtype):
-            picked = tile(name, [P, offsets.shape[1] * LIST_ROWS], dtype)
+        def gather(name, window, offsets, dtype, tag=None):
+            picked = tile(name, [P, offsets.shape[1] * LIST_ROWS], dtype, tag)
             nc.vector.tensor_copy(picked[:], window.indirect(offsets[:]))
             return picked
 
-        def deal(name, source, dtype):
-            dealt = tile(name, [P, H], dtype)
+        def deal(dealt, source):
             nc.vector.tensor_copy(
-                dealt[:].bitcast(U32).rearrange("p (t g r) -> p t g r", t=PACK, g=BLOCKS),
-                source[:].bitcast(U32).rearrange("p (g t r) -> p t g r", t=PACK, g=BLOCKS),
+                dealt.bitcast(U32).rearrange("p (t g r) -> p t g r", t=PACK, g=BLOCKS),
+                source.bitcast(U32).rearrange("p (g t r) -> p t g r", t=PACK, g=BLOCKS),
             )
-            return dealt
 
         def word_order(grouped):
             return grouped[:].rearrange("p (c i t) -> p c t i", i=RUN, t=PACK)
@@ -84,24 +81,22 @@ def tile_picked_kmixgpairkdif_none_p_kernel(
                 stop=stop,
             )
 
+        def load_scales(name, source):
+            table = tile(name, [P, source.shape[2]], U8)
+            rows = source[0].bitcast(I32)
+            nc.sync.dma_start(table[:].bitcast(I32), rows.unsqueeze(1).broadcast_to([BLOCKS, P // BLOCKS, rows.shape[1]]))
+            return table
+
         k1_sb = load_list("k1_sb", k1)
-        d_scale_table = tile("d_scale_table", [P, G], U8)
-        nc.sync.dma_start(
-            d_scale_table[:].bitcast(I32), d_scales[0].bitcast(I32).unsqueeze(1).broadcast_to([16, 8, G // 4])
-        )
+        d_scale_table = load_scales("d_scale_table", d_scales)
         offs_sb = load_list("offs_sb", offs)
+        x_scale_table = load_scales("x_scale_table", x_scales)
         two_sb = load_list("two_sb", two)
         n1_sb = load_list("n1_sb", n1)
-        n3_sb = load_list("n3_sb", n3)
-        n2_sb = load_list("n2_sb", n2)
         d_word_table = load_words("d_word_table", d_words)
         x_word_table = load_words("x_word_table", x_words)
-        x_scale_table = tile("x_scale_table", [P, T], U8)
-        nc.vector.memset(x_scale_table[:].bitcast(I32), 0)
-        for q in range(4):
-            nc.scalar.dma_start(
-                x_scale_table[32 * q : 32 * q + 4, :].bitcast(I32), x_scales[0, 4 * q : 4 * q + 4, :].bitcast(I32)
-            )
+        n3_sb = load_list("n3_sb", n3)
+        n2_sb = load_list("n2_sb", n2)
 
         scores = [tile(f"scores{t}", [P, S + SCORE_SPARE], F32) for t in range(PACK)]
         for t in range(PACK):
@@ -110,33 +105,39 @@ def tile_picked_kmixgpairkdif_none_p_kernel(
         for m in range(0, N // P, 2):
             nc.gpsimd.memset(results[m][:, S:], 0.0)
 
-        key_scales_picked = gather("key_scales_picked", d_scale_table[:], k1_sb, U8)
-        key_scales = deal("key_scales", key_scales_picked, U8)
-        for i in range(1, 4):
-            nc.scalar.dma_start(key_scales[i:P:32, :].bitcast(I32), key_scales[8 * i : P : 32, :].bitcast(I32))
-        token_scales = gather("token_scales", x_scale_table[:], offs_sb, U8)
-        key_words_picked = gather("key_words_picked", d_word_table[:].bitcast(U32), k1_sb, U32)
-        key_words = deal("key_words", key_words_picked, U32)
-        w2_raw = tile("w2_raw", [P, PACK, N], F32, tag="d_word_table")
+        picked_scales = tile("picked_scales", [P, H + 2 * S], U8)
+        planes = tile("planes", [P, H + 2 * S], U8)
+        nc.gpsimd.memset(planes[:].bitcast(I32), 0)
+        nc.vector.tensor_copy(picked_scales[:, :H], d_scale_table[:].indirect(k1_sb[:]))
+        nc.vector.tensor_copy(picked_scales[:, H : H + S], x_scale_table[:].indirect(offs_sb[:]))
+        nc.vector.tensor_copy(picked_scales[:, H + S :], x_scale_table[:].indirect(two_sb[:]))
+        for q in range(4):
+            nc.sync.dma_start(
+                planes[32 * q : 32 * q + 4, :].bitcast(I32), picked_scales[32 * q : 32 * q + 32 : 8, :].bitcast(I32)
+            )
+        token_scales, second_scales = planes[:, H : H + S], planes[:, H + S :]
+        w2_raw = tile("w2_raw", [P, PACK, N], F32, tag="x_scale_table")
         nc.sync.dma_start(w2_raw[:], w2.rearrange("(p t) n -> p t n", t=PACK))
-        gains = tile("gains", [P, PACK, 8], F32, tag="key_words_picked")
+
+        key_words = tile("key_words", [P, H], U32)
+        deal(key_words[:], gather("key_words_picked", d_word_table[:].bitcast(U32), k1_sb, U32)[:])
+        token_words = gather("token_words", x_word_table[:].bitcast(U32), offs_sb, U32)
+        key_scales = tile("key_scales", [P, H], U8)
+        deal(key_scales[:], planes[:, :H])
+        gains = tile("gains", [P, PACK, 8], F32, tag="d_word_table")
         for t in range(PACK):
             nc.sync.dma_start(gains[:, t, 0:1], gn.rearrange("(g t r) o -> t g r o", t=PACK, g=BLOCKS)[t])
-        token_words = gather("token_words", x_word_table[:].bitcast(U32), offs_sb, U32)
+        w1_raw = tile("w1_raw", [P, PACK, N], F32, tag="key_words_picked")
+        for t in range(PACK):
+            nc.sync.dma_start(w1_raw[:, t, :], w1.rearrange("(g t r) n -> t g r n", t=PACK, g=BLOCKS)[t])
 
         for t in range(PACK):
             acc = psum.tile([P, S], F32, name=f"score_acc{t}", tag=f"bank{t}")
             multiply(acc[:], (key_words, key_scales), slice(t * P, (t + 1) * P), (token_words, token_scales), slice(0, S), True, True)
             nc.scalar.activation(scores[t][:, :S], acc[:], COPY, scale=0.0625)
 
-        second = (
-            gather("second_words", x_word_table[:].bitcast(U32), two_sb, U32),
-            gather("second_scales", x_scale_table[:], two_sb, U8),
-        )
+        second = (gather("second_words", x_word_table[:].bitcast(U32), two_sb, U32, "picked_scales"), second_scales)
 
-        w1_raw = tile("w1_raw", [P, PACK, N], F32, tag="x_scale_table")
-        for t in range(PACK):
-            nc.sync.dma_start(w1_raw[:, t, :], w1.rearrange("(g t r) n -> t g r n", t=PACK, g=BLOCKS)[t])
         w2_grouped = tile("w2_grouped", [P, PACK * N], BF16)
         nc.vector.tensor_copy(word_order(w2_grouped), plane_order(w2_raw[:]))
         w2_mx = quantize("w2", w2_grouped)
@@ -148,20 +149,23 @@ def tile_picked_kmixgpairkdif_none_p_kernel(
         last = len(spans) - 1
         early = spans[last].start
 
-        w1_grouped = tile("w1_grouped", [P, PACK * N], BF16)
         members = []
         for c, cols in enumerate(spans):
             pair_offsets = n1_sb[:, 2 * cols.start // LIST_ROWS : 2 * cols.stop // LIST_ROWS]
             members.append(tile(f"members{c}", [P, PACK, 2 * CHUNKS[c]], F32))
-            if c == last:
-                nc.scalar.copy(word_order(w1_grouped), plane_order(w1_raw[:]))
             for t in range(PACK):
-                if c == 0 and t < VECTOR_GATHERS:
+                if t == 0:
                     nc.vector.tensor_copy(members[c][:, t, :], scores[t][:].indirect(pair_offsets))
                 else:
                     nc.scalar.activation(members[c][:, t, :], scores[t][:].indirect(pair_offsets), COPY)
 
+        half = N // 2
+        w1_grouped = [tile(f"w1_grouped{u}", [P, PACK * half], BF16) for u in range(2)]
+        for u in range(2):
+            nc.scalar.copy(word_order(w1_grouped[u]), plane_order(w1_raw[:, :, u * half : (u + 1) * half]))
+
         z_mx = []
+        w1_mx = []
         for c, cols in enumerate(spans):
             width = CHUNKS[c]
             larger = tile(f"larger{c}", [P, PACK, width], F32)
@@ -176,26 +180,35 @@ def tile_picked_kmixgpairkdif_none_p_kernel(
             spread_gains = gains[:, :, 0:1].unsqueeze(1).broadcast_to([P, width // RUN, PACK, RUN])
             nc.vector.tensor_tensor(word_order(z_grouped), plane_order(rest[:]), spread_gains, ALU.mult)
             z_mx.append(quantize(f"z{c}", z_grouped))
-            if c == last - 1:
-                w1_mx = quantize("w1", w1_grouped)
+            if c >= last - 1:
+                w1_mx.append(quantize(f"w1_{len(w1_mx)}", w1_grouped[len(w1_mx)]))
 
         order = (1, 0, 3, 2)
-        early_acc = {m: psum.tile([P, early], F32, name=f"early_acc{m}", tag=f"bank{PACK + m}") for m in order}
-        last_acc = {m: psum.tile([P, S - early], F32, name=f"last_acc{m}", tag=f"bank{m}") for m in order}
+        copy_out = (nc.vector.tensor_copy, nc.scalar.copy)
+        accs = {m: psum.tile([P, early if m < 2 else S], F32, name=f"acc{m}", tag=f"bank{PACK + m}") for m in order}
+        last_accs = {m: psum.tile([P, S - early], F32, name=f"last_acc{m}", tag=f"bank{m}") for m in order[:2]}
 
         def target(c, m):
-            return last_acc[m][:] if c == last else early_acc[m][:, spans[c]]
+            return last_accs[m][:] if c == last and m < 2 else accs[m][:, spans[c]]
 
         for m in order:
-            for c, cols in enumerate(spans):
-                multiply(target(c, m), w2_mx, slice(m * P, (m + 1) * P), second, cols, c in (0, last), False)
-        for c, cols in enumerate(spans):
-            for m in order:
-                multiply(target(c, m), w1_mx, slice(m * P, (m + 1) * P), z_mx[c], slice(0, CHUNKS[c]), False, c >= last - 1)
-                if c == last - 1:
-                    nc.scalar.copy(results[m][:, :early], early_acc[m][:])
-                if c == last:
-                    (nc.scalar.copy if m % 2 else nc.vector.tensor_copy)(results[m][:, early:S], last_acc[m][:])
+            rows = slice(m * P, (m + 1) * P)
+            if m < 2:
+                for c, cols in enumerate(spans):
+                    multiply(target(c, m), w2_mx, rows, second, cols, c in (0, last), False)
+            else:
+                multiply(accs[m][:], w2_mx, rows, second, slice(0, S), True, False)
+        for u in range(2):
+            for c in range(len(spans)):
+                for m in order[2 * u : 2 * u + 2]:
+                    closes = c == last or (u == 0 and c == last - 1)
+                    multiply(target(c, m), w1_mx[u], slice(m % 2 * P, (m % 2 + 1) * P), z_mx[c], slice(0, CHUNKS[c]), False, closes)
+                    if u == 0 and c == last - 1:
+                        nc.scalar.copy(results[m][:, :early], accs[m][:])
+                    if u == 0 and c == last:
+                        copy_out[m % 2](results[m][:, early:S], last_accs[m][:])
+                    if u == 1 and c == last:
+                        copy_out[m % 2](results[m][:, :S], accs[m][:])
 
         partners = {}
         for m in (1, 0, 3, 2):

@@ -48,7 +48,7 @@ def tile_picked_kmixgpairkdif_none_p_kernel(
 
         def gather(name, window, offsets, dtype, tag=None):
             picked = tile(name, [P, offsets.shape[1] * LIST_ROWS], dtype, tag)
-            nc.vector.tensor_copy(picked[:], window.indirect(offsets[:]))
+            nc.vector.tensor_copy(picked[:], window.indirect(offsets))
             return picked
 
         def deal(dealt, source):
@@ -120,10 +120,14 @@ def tile_picked_kmixgpairkdif_none_p_kernel(
         nc.sync.dma_start(w2_raw[:], w2.rearrange("(p t) n -> p t n", t=PACK))
 
         key_words = tile("key_words", [P, H], U32)
-        deal(key_words[:], gather("key_words_picked", d_word_table[:].bitcast(U32), k1_sb, U32)[:])
-        token_words = gather("token_words", x_word_table[:].bitcast(U32), offs_sb, U32)
+        deal(key_words[:], gather("key_words_picked", d_word_table[:].bitcast(U32), k1_sb[:], U32)[:])
         key_scales = tile("key_scales", [P, H], U8)
-        deal(key_scales[:], planes[:, :H])
+        token_words = []
+        for u in range(2):
+            offsets = offs_sb[:, u * S // 2 // LIST_ROWS : (u + 1) * S // 2 // LIST_ROWS]
+            token_words.append(gather(f"token_words{u}", x_word_table[:].bitcast(U32), offsets, U32))
+            if u == 0:
+                deal(key_scales[:], planes[:, :H])
         gains = tile("gains", [P, PACK, 8], F32, tag="d_word_table")
         for t in range(PACK):
             nc.sync.dma_start(gains[:, t, 0:1], gn.rearrange("(g t r) o -> t g r o", t=PACK, g=BLOCKS)[t])
@@ -131,12 +135,15 @@ def tile_picked_kmixgpairkdif_none_p_kernel(
         for t in range(PACK):
             nc.sync.dma_start(w1_raw[:, t, :], w1.rearrange("(g t r) n -> t g r n", t=PACK, g=BLOCKS)[t])
 
-        for t in range(PACK):
-            acc = psum.tile([P, S], F32, name=f"score_acc{t}", tag=f"bank{t}")
-            multiply(acc[:], (key_words, key_scales), slice(t * P, (t + 1) * P), (token_words, token_scales), slice(0, S), True, True)
-            nc.scalar.activation(scores[t][:, :S], acc[:], COPY, scale=0.0625)
+        for u in range(2):
+            cols = slice(u * S // 2, (u + 1) * S // 2)
+            for t in range(PACK):
+                acc = psum.tile([P, S // 2], F32, name=f"score_acc{u}_{t}", tag=f"bank{PACK * u + t}")
+                tokens = (token_words[u], token_scales[:, cols])
+                multiply(acc[:], (key_words, key_scales), slice(t * P, (t + 1) * P), tokens, slice(0, S // 2), True, True)
+                nc.scalar.activation(scores[t][:, cols], acc[:], COPY, scale=0.0625)
 
-        second = (gather("second_words", x_word_table[:].bitcast(U32), two_sb, U32, "picked_scales"), second_scales)
+        second = (gather("second_words", x_word_table[:].bitcast(U32), two_sb[:], U32, "picked_scales"), second_scales)
 
         w2_grouped = tile("w2_grouped", [P, PACK * N], BF16)
         nc.vector.tensor_copy(word_order(w2_grouped), plane_order(w2_raw[:]))
@@ -152,12 +159,13 @@ def tile_picked_kmixgpairkdif_none_p_kernel(
         members = []
         for c, cols in enumerate(spans):
             pair_offsets = n1_sb[:, 2 * cols.start // LIST_ROWS : 2 * cols.stop // LIST_ROWS]
-            members.append(tile(f"members{c}", [P, PACK, 2 * CHUNKS[c]], F32))
+            members.append(tile(f"members{c}", [P, PACK * 2 * CHUNKS[c]], F32))
             for t in range(PACK):
-                if t == 0:
-                    nc.vector.tensor_copy(members[c][:, t, :], scores[t][:].indirect(pair_offsets))
+                fetched = members[c][:, 2 * CHUNKS[c] * t : 2 * CHUNKS[c] * (t + 1)]
+                if t == 0 and c < last:
+                    nc.vector.tensor_copy(fetched, scores[t][:].indirect(pair_offsets))
                 else:
-                    nc.scalar.activation(members[c][:, t, :], scores[t][:].indirect(pair_offsets), COPY)
+                    nc.scalar.activation(fetched, scores[t][:].indirect(pair_offsets), COPY)
 
         half = N // 2
         w1_grouped = [tile(f"w1_grouped{u}", [P, PACK * half], BF16) for u in range(2)]
@@ -168,47 +176,45 @@ def tile_picked_kmixgpairkdif_none_p_kernel(
         w1_mx = []
         for c, cols in enumerate(spans):
             width = CHUNKS[c]
-            larger = tile(f"larger{c}", [P, PACK, width], F32)
-            pairs = members[c][:].rearrange("p t (j e) -> p t j e", e=2)
+            larger = tile(f"larger{c}", [P, PACK * width], F32)
+            firsts, seconds = members[c][:, 0::2], members[c][:, 1::2]
             for t in range(PACK):
-                nc.vector.tensor_tensor(larger[:, t, :], pairs[:, t, :, 0], scores[t][:, cols], ALU.max)
-            excess = tile(f"excess{c}", [P, PACK, width], F32)
-            nc.vector.tensor_tensor(excess[:], pairs[:, :, :, 1], larger[:], ALU.subtract)
-            rest = tile(f"rest{c}", [P, PACK, width], F32)
-            nc.vector.scalar_tensor_tensor(rest[:], excess[:], 0.0, pairs[:, :, :, 0], ALU.min, ALU.add)
+                part = slice(t * width, (t + 1) * width)
+                nc.vector.tensor_tensor(larger[:, part], firsts[:, part], scores[t][:, cols], ALU.max)
+            excess = tile(f"excess{c}", [P, PACK * width], F32)
+            nc.vector.tensor_tensor(excess[:], seconds, larger[:], ALU.subtract)
+            if c == last:
+                w1_mx.append(quantize("w1_0", w1_grouped[0]))
+            rest = tile(f"rest{c}", [P, PACK * width], F32)
+            nc.vector.scalar_tensor_tensor(rest[:], excess[:], 0.0, firsts, ALU.min, ALU.add)
+            if c == last:
+                w1_mx.append(quantize("w1_1", w1_grouped[1]))
             z_grouped = tile(f"z_grouped{c}", [P, PACK * width], BF16)
             spread_gains = gains[:, :, 0:1].unsqueeze(1).broadcast_to([P, width // RUN, PACK, RUN])
-            nc.vector.tensor_tensor(word_order(z_grouped), plane_order(rest[:]), spread_gains, ALU.mult)
+            nc.vector.tensor_tensor(word_order(z_grouped), plane_order(rest[:].rearrange("p (t j) -> p t j", t=PACK)), spread_gains, ALU.mult)
             z_mx.append(quantize(f"z{c}", z_grouped))
-            if c >= last - 1:
-                w1_mx.append(quantize(f"w1_{len(w1_mx)}", w1_grouped[len(w1_mx)]))
 
         order = (1, 0, 3, 2)
         copy_out = (nc.vector.tensor_copy, nc.scalar.copy)
-        accs = {m: psum.tile([P, early if m < 2 else S], F32, name=f"acc{m}", tag=f"bank{PACK + m}") for m in order}
-        last_accs = {m: psum.tile([P, S - early], F32, name=f"last_acc{m}", tag=f"bank{m}") for m in order[:2]}
+        early_accs = {m: psum.tile([P, early], F32, name=f"early_acc{m}", tag=f"bank{PACK + m}") for m in order}
+        last_accs = {m: psum.tile([P, S - early], F32, name=f"last_acc{m}", tag=f"bank{m}") for m in order}
 
         def target(c, m):
-            return last_accs[m][:] if c == last and m < 2 else accs[m][:, spans[c]]
+            return last_accs[m][:] if c == last else early_accs[m][:, spans[c]]
+
+        def add_z(c, m):
+            multiply(target(c, m), w1_mx[m // 2], slice(m % 2 * P, (m % 2 + 1) * P), z_mx[c], slice(0, CHUNKS[c]), False, c >= last - 1)
 
         for m in order:
-            rows = slice(m * P, (m + 1) * P)
-            if m < 2:
-                for c, cols in enumerate(spans):
-                    multiply(target(c, m), w2_mx, rows, second, cols, c in (0, last), False)
-            else:
-                multiply(accs[m][:], w2_mx, rows, second, slice(0, S), True, False)
-        for u in range(2):
-            for c in range(len(spans)):
-                for m in order[2 * u : 2 * u + 2]:
-                    closes = c == last or (u == 0 and c == last - 1)
-                    multiply(target(c, m), w1_mx[u], slice(m % 2 * P, (m % 2 + 1) * P), z_mx[c], slice(0, CHUNKS[c]), False, closes)
-                    if u == 0 and c == last - 1:
-                        nc.scalar.copy(results[m][:, :early], accs[m][:])
-                    if u == 0 and c == last:
-                        copy_out[m % 2](results[m][:, early:S], last_accs[m][:])
-                    if u == 1 and c == last:
-                        copy_out[m % 2](results[m][:, :S], accs[m][:])
+            for c, cols in enumerate(spans):
+                multiply(target(c, m), w2_mx, slice(m * P, (m + 1) * P), second, cols, c in (0, last), False)
+        for m in order:
+            for c in range(last):
+                add_z(c, m)
+            nc.scalar.copy(results[m][:, :early], early_accs[m][:])
+        for m in order:
+            add_z(last, m)
+            copy_out[m % 2](results[m][:, early:S], last_accs[m][:])
 
         partners = {}
         for m in (1, 0, 3, 2):

from contextlib import ExitStack

import concourse.mybir as mybir

K, T, S, N, G, H, W, U = 512, 2048, 512, 512, 2048, 512, 1024, 384
FLOPS = 2 * K * H * S + 2 * H * N * S + 2 * K * N * S

F32 = mybir.dt.float32
BF16 = mybir.dt.bfloat16
I32 = mybir.dt.int32
U32 = mybir.dt.uint32
U16 = mybir.dt.uint16
U8 = mybir.dt.uint8
FP8X4 = mybir.dt.float8_e4m3fn_x4
ALU = mybir.AluOpType
COPY = mybir.ActivationFunctionType.Copy

P = 128
PACK = 4
LIST_ROWS = 16
BLOCKS = 16
RUN = 4
CHUNKS = (128, 256, 128)
SCORE_SPARE = 32
OUT_SPARE = 256


def tile_picked_kmixgpairkdif_none_p_kernel(
    tc, x_words, x_scales, d_words, d_scales, gn, w1, w2, offs, k1, n1, two, n2, n3, out
):
    nc = tc.nc
    with ExitStack() as ctx:
        keep = ctx.enter_context(tc.tile_pool(name="keep", bufs=1))
        psum = ctx.enter_context(tc.psum_pool(name="psum", bufs=1))

        def tile(name, shape, dtype, tag=None):
            return keep.tile(shape, dtype, name=name, tag=tag or name, align_bytes=64)

        def load_list(name, source):
            offsets = tile(name, list(source.shape), U16)
            nc.sync.dma_start(offsets[:], source)
            return offsets

        def load_words(name, source):
            words = tile(name, [P, source.shape[2]], I32)
            nc.sync.dma_start(words[:], source[0].rearrange("p n t -> p (n t)").bitcast(I32))
            return words

        def gather(name, window, offsets, dtype, tag=None):
            picked = tile(name, [P, offsets.shape[1] * LIST_ROWS], dtype, tag)
            nc.vector.tensor_copy(picked[:], window.indirect(offsets))
            return picked

        def deal(dealt, source):
            nc.vector.tensor_copy(
                dealt.bitcast(U32).rearrange("p (t g r) -> p t g r", t=PACK, g=BLOCKS),
                source.bitcast(U32).rearrange("p (g t r) -> p t g r", t=PACK, g=BLOCKS),
            )

        def word_order(grouped):
            return grouped[:].rearrange("p (c i t) -> p c t i", i=RUN, t=PACK)

        def plane_order(planes):
            return planes.rearrange("p t (c i) -> p c t i", i=RUN)

        def quantize(name, grouped):
            width = grouped.shape[1] // PACK
            codes = tile(name + "_codes", [P, width], U32)
            scales = tile(name + "_scales", [P, width], U8)
            nc.vector.quantize_mx(out=codes[:].bitcast(FP8X4), scales=scales[:], in_=grouped[:])
            return codes, scales

        def multiply(acc, left, left_cols, right, right_cols, start, stop):
            nc.tensor.matmul_mx(
                out=acc,
                lhsT=left[0][:, left_cols].bitcast(FP8X4),
                lhsT_scale=left[1][:, left_cols],
                rhs=right[0][:, right_cols].bitcast(FP8X4),
                rhs_scale=right[1][:, right_cols],
                start=start,
                stop=stop,
            )

        def load_scales(name, source):
            table = tile(name, [P, source.shape[2]], U8)
            rows = source[0].bitcast(I32)
            nc.sync.dma_start(table[:].bitcast(I32), rows.unsqueeze(1).broadcast_to([BLOCKS, P // BLOCKS, rows.shape[1]]))
            return table

        k1_sb = load_list("k1_sb", k1)
        d_scale_table = load_scales("d_scale_table", d_scales)
        offs_sb = load_list("offs_sb", offs)
        x_scale_table = load_scales("x_scale_table", x_scales)
        two_sb = load_list("two_sb", two)
        n1_sb = load_list("n1_sb", n1)
        d_word_table = load_words("d_word_table", d_words)
        x_word_table = load_words("x_word_table", x_words)
        n3_sb = load_list("n3_sb", n3)
        n2_sb = load_list("n2_sb", n2)

        scores = [tile(f"scores{t}", [P, S + SCORE_SPARE], F32) for t in range(PACK)]
        for t in range(PACK):
            nc.gpsimd.memset(scores[t][:, S:], 0.0)
        results = [tile(f"results{m}", [P, S + OUT_SPARE * (1 - m % 2)], F32) for m in range(N // P)]
        for m in range(0, N // P, 2):
            nc.gpsimd.memset(results[m][:, S:], 0.0)

        picked_scales = tile("picked_scales", [P, H + 2 * S], U8)
        planes = tile("planes", [P, H + 2 * S], U8)
        nc.gpsimd.memset(planes[:].bitcast(I32), 0)
        nc.vector.tensor_copy(picked_scales[:, :H], d_scale_table[:].indirect(k1_sb[:]))
        nc.vector.tensor_copy(picked_scales[:, H : H + S], x_scale_table[:].indirect(offs_sb[:]))
        nc.vector.tensor_copy(picked_scales[:, H + S :], x_scale_table[:].indirect(two_sb[:]))
        for q in range(4):
            nc.sync.dma_start(
                planes[32 * q : 32 * q + 4, :].bitcast(I32), picked_scales[32 * q : 32 * q + 32 : 8, :].bitcast(I32)
            )
        token_scales, second_scales = planes[:, H : H + S], planes[:, H + S :]
        w2_raw = tile("w2_raw", [P, PACK, N], F32, tag="x_scale_table")
        nc.sync.dma_start(w2_raw[:], w2.rearrange("(p t) n -> p t n", t=PACK))

        key_words = tile("key_words", [P, H], U32)
        deal(key_words[:], gather("key_words_picked", d_word_table[:].bitcast(U32), k1_sb[:], U32)[:])
        key_scales = tile("key_scales", [P, H], U8)
        token_words = []
        for u in range(2):
            offsets = offs_sb[:, u * S // 2 // LIST_ROWS : (u + 1) * S // 2 // LIST_ROWS]
            token_words.append(gather(f"token_words{u}", x_word_table[:].bitcast(U32), offsets, U32))
            if u == 0:
                deal(key_scales[:], planes[:, :H])
        gains = tile("gains", [P, PACK, 8], F32, tag="d_word_table")
        for t in range(PACK):
            nc.sync.dma_start(gains[:, t, 0:1], gn.rearrange("(g t r) o -> t g r o", t=PACK, g=BLOCKS)[t])
        w1_raw = tile("w1_raw", [P, PACK, N], F32, tag="key_words_picked")
        for t in range(PACK):
            nc.sync.dma_start(w1_raw[:, t, :], w1.rearrange("(g t r) n -> t g r n", t=PACK, g=BLOCKS)[t])

        for u in range(2):
            cols = slice(u * S // 2, (u + 1) * S // 2)
            for t in range(PACK):
                acc = psum.tile([P, S // 2], F32, name=f"score_acc{u}_{t}", tag=f"bank{PACK * u + t}")
                tokens = (token_words[u], token_scales[:, cols])
                multiply(acc[:], (key_words, key_scales), slice(t * P, (t + 1) * P), tokens, slice(0, S // 2), True, True)
                nc.scalar.activation(scores[t][:, cols], acc[:], COPY, scale=0.0625)

        second = (gather("second_words", x_word_table[:].bitcast(U32), two_sb[:], U32, "picked_scales"), second_scales)

        w2_grouped = tile("w2_grouped", [P, PACK * N], BF16)
        nc.vector.tensor_copy(word_order(w2_grouped), plane_order(w2_raw[:]))
        w2_mx = quantize("w2", w2_grouped)

        spans = []
        for width in CHUNKS:
            first = sum(span.stop - span.start for span in spans)
            spans.append(slice(first, first + width))
        last = len(spans) - 1
        early = spans[last].start

        members = []
        for c, cols in enumerate(spans):
            pair_offsets = n1_sb[:, 2 * cols.start // LIST_ROWS : 2 * cols.stop // LIST_ROWS]
            members.append(tile(f"members{c}", [P, PACK * 2 * CHUNKS[c]], F32))
            for t in range(PACK):
                fetched = members[c][:, 2 * CHUNKS[c] * t : 2 * CHUNKS[c] * (t + 1)]
                if t == 0 and c < last:
                    nc.vector.tensor_copy(fetched, scores[t][:].indirect(pair_offsets))
                else:
                    nc.scalar.activation(fetched, scores[t][:].indirect(pair_offsets), COPY)

        half = N // 2
        w1_grouped = [tile(f"w1_grouped{u}", [P, PACK * half], BF16) for u in range(2)]
        for u in range(2):
            nc.scalar.copy(word_order(w1_grouped[u]), plane_order(w1_raw[:, :, u * half : (u + 1) * half]))

        z_mx = []
        w1_mx = []
        for c, cols in enumerate(spans):
            width = CHUNKS[c]
            larger = tile(f"larger{c}", [P, PACK * width], F32)
            firsts, seconds = members[c][:, 0::2], members[c][:, 1::2]
            for t in range(PACK):
                part = slice(t * width, (t + 1) * width)
                nc.vector.tensor_tensor(larger[:, part], firsts[:, part], scores[t][:, cols], ALU.max)
            excess = tile(f"excess{c}", [P, PACK * width], F32)
            nc.vector.tensor_tensor(excess[:], seconds, larger[:], ALU.subtract)
            if c == last:
                w1_mx.append(quantize("w1_0", w1_grouped[0]))
            rest = tile(f"rest{c}", [P, PACK * width], F32)
            nc.vector.scalar_tensor_tensor(rest[:], excess[:], 0.0, firsts, ALU.min, ALU.add)
            if c == last:
                w1_mx.append(quantize("w1_1", w1_grouped[1]))
            z_grouped = tile(f"z_grouped{c}", [P, PACK * width], BF16)
            spread_gains = gains[:, :, 0:1].unsqueeze(1).broadcast_to([P, width // RUN, PACK, RUN])
            nc.vector.tensor_tensor(word_order(z_grouped), plane_order(rest[:].rearrange("p (t j) -> p t j", t=PACK)), spread_gains, ALU.mult)
            z_mx.append(quantize(f"z{c}", z_grouped))

        order = (1, 0, 3, 2)
        copy_out = (nc.vector.tensor_copy, nc.scalar.copy)
        early_accs = {m: psum.tile([P, early], F32, name=f"early_acc{m}", tag=f"bank{PACK + m}") for m in order}
        last_accs = {m: psum.tile([P, S - early], F32, name=f"last_acc{m}", tag=f"bank{m}") for m in order}

        def target(c, m):
            return last_accs[m][:] if c == last else early_accs[m][:, spans[c]]

        def add_z(c, m):
            multiply(target(c, m), w1_mx[m // 2], slice(m % 2 * P, (m % 2 + 1) * P), z_mx[c], slice(0, CHUNKS[c]), False, c >= last - 1)

        for m in order:
            for c, cols in enumerate(spans):
                multiply(target(c, m), w2_mx, slice(m * P, (m + 1) * P), second, cols, c in (0, last), False)
        for m in order:
            for c in range(last):
                add_z(c, m)
            nc.scalar.copy(results[m][:, :early], early_accs[m][:])
        for m in order:
            add_z(last, m)
            copy_out[m % 2](results[m][:, early:S], last_accs[m][:])

        partners = {}
        for m in (1, 0, 3, 2):
            partners[m] = tile(f"partner{m}", [P, U], F32)
            nc.scalar.activation(partners[m][:], results[m][:].indirect(n3_sb[:]), COPY, scale=-0.5)
        for m in (0, 2):
            old = tile(f"old{m}", [P, U], F32)
            nc.vector.tensor_copy(old[:], results[m][:].indirect(n2_sb[:]))
            new = tile(f"new{m + 1}", [P, U], F32)
            nc.vector.tensor_tensor(new[:], results[m + 1][:].indirect(n2_sb[:]), partners[m + 1][:], ALU.add)
            nc.scalar.activation(results[m + 1][:].indirect(n2_sb[:]), new[:], COPY)
            nc.vector.tensor_tensor(results[m][:].indirect(n2_sb[:]), old[:], partners[m][:], ALU.add)
        for m in range(N // P):
            nc.sync.dma_start(out[m * P : (m + 1) * P, :], results[m][:, :S])
